import numpy as np, ml_dtypes
CORES = [23,119,17,113]
N = 4
import mx_ref
BF = ml_dtypes.bfloat16
def f(rng, *shape):
    return mx_ref.flush((rng.standard_normal(shape, dtype=np.float32) * np.exp2(rng.integers(-2, 3, shape[:-1] + (1,)))).astype(BF))
def wide(rng, *shape, cols=0):
    v = rng.standard_normal(shape, dtype=np.float32) * np.exp2(rng.integers(-12, 13, shape)).astype(np.float32)
    if cols: v *= np.repeat(np.exp2(rng.integers(-cols, cols + 1, shape[:-2] + (1, shape[-1] // 4))) * (rng.random(shape[:-2] + (1, shape[-1] // 4)) > 0.0625), 4, axis=-1).astype(np.float32)
    return mx_ref.flush(v.astype(BF))
R, XC = 2048, 384
def lists(rng):
    return rng.integers(0, R, (N, N, 512))
def picks(L):
    return np.ascontiguousarray(L.reshape(N, N, 128, 4).transpose(0, 2, 1, 3)).reshape(N, 128, 4 * N).astype(np.int32)
def setup_inputs(rng):
    return {"x": f(rng, N, R, XC), "w": f(rng, N, R, 128), "pick": picks(lists(rng))}
def setup_inputs_alike(rng):
    d = setup_inputs(rng); L = lists(rng)
    L[:] = L[0, 0].copy()
    d["pick"] = picks(L); return d
def setup_inputs_giant(rng):
    d = setup_inputs(rng); L = lists(rng); big = {}
    for n in ("x", "w"):
        big[n] = 32 * np.arange(R // 32) + rng.integers(0, 32, (N, R // 32))
        m = np.ones((N, R, 1), np.float32)
        for r in range(N): m[r, big[n][r]] = 4096
        d[n] = (d[n].astype(np.float32) * m).astype(BF)
    for r in range(N):
        for s in range(N):
            for g in range(16):
                a, b = 32 * g + rng.permutation(32)[:2]
                L[r, s, a] = rng.choice(big["x"][s]); L[r, s, b] = rng.choice(big["w"][r])
    d["pick"] = picks(L); return d
def setup_inputs_repeat(rng):
    d = setup_inputs(rng); L = lists(rng)
    for r in range(N): L[r, (r + rng.integers(1, N)) % N] = rng.integers(0, R)
    d["pick"] = picks(L); return d
def setup_inputs_sorted(rng):
    d = setup_inputs(rng); L = lists(rng)
    L[:, :, 0] = 0; L[:, :, 1] = R - 1
    d["pick"] = picks(np.sort(L, axis=2)); return d
def setup_inputs_spread(rng):
    d = setup_inputs(rng); d["x"] = wide(rng, N, R, XC); d["w"] = wide(rng, N, R, 128); return d
def check_inputs(d):
    b = []
    for n in ("x", "w"):
        a = np.abs(np.asarray(d[n]).astype(np.float32))
        if not np.isfinite(a).all() or ((a != 0) & ((a < 2.0 ** -30) | (a > 2.0 ** 30))).any(): b.append(n)
    if d["pick"].min() < 0 or d["pick"].max() >= R: b.append("pick")
    return b
def rowtile(v, k):
    return np.ascontiguousarray(v[k].transpose(0, 2, 1)).reshape(128, -1)
def reference(x, w, pick):
    y = np.zeros((N, 128, N * XC), np.float32)
    for r in range(N):
        for s in range(N):
            k = pick[r][:, 4 * s:4 * s + 4]
            y[r][:, XC * s:XC * s + XC] = mx_ref.matmul(mx_ref.quantize(rowtile(w[r], k)), mx_ref.quantize(rowtile(x[s], k)))
    return {"y": y}

@@ -1,0 +1,322 @@
+from concourse.bass import DstId, IndirectOffsetOnAxis, RemoteDMATransfer
+from concourse.mybir import dt, AluOpType, ActivationFunctionType
+
+N, R, XC = 4, 2048, 384
+COPY = ActivationFunctionType.Copy
+XW = 6144
+XSLOT = 768
+WSLOT = 512
+
+PLAN = """
+G:o1 G:i0 G:o0 G:o2
+Y:lw S:g12 P:p12 S:g20 V:g10 V:tw S:g22 V:g21 S:g11 P:p10 V:l00 P:p11 S:e10 V:m2 V:e11 S:l01 V:l02
+S:gw0 P:pw0 V:l03 S:gw1 V:q0 G:s0 V:ew0 V:e12 S:gw3 P:pw1 V:q1 P:pw3 S:l31 S:gw2 Y:cw S:l30 V:ew1 P:pw2
+Y:d2 V:ew3 V:q2 G:o3 S:l32 V:ew2 S:l33 V:qw S:y0 G:s1 V:q3 V:y3 V:y1 V:y2 G:s2
+"""
+
+SCRATCH = {
+    "ones": ("sbuf", [128, 128], "float32"),
+    "ident": ("sbuf", [128, 128], "float32"),
+    "pk": ("sbuf", [128, 16], "int32"),
+    "ld": ("sbuf", [128, 4], "int32"),
+    "la": ("sbuf", [128, 2, 4], "float32"),
+    "fx": ("sbuf", [128, 16], "float32"),
+    "fw": ("sbuf", [128, 16], "float32"),
+    "nat": ("sbuf", [128, 48, 128], "bfloat16"),
+    "stg": ("sbuf", [128, XW], "bfloat16"),
+    "xw": ("sbuf", [128, XW], "bfloat16"),
+    "wn": ("sbuf", [128, 16, 128], "bfloat16"),
+    "wst": ("sbuf", [128, 2048], "bfloat16"),
+    "ww": ("sbuf", [128, 2048], "bfloat16"),
+    "wt": ("sbuf", [128, 2048], "bfloat16"),
+    "wq": ("sbuf", [128, 512], "float8_e4m3fn_x4"),
+    "ws": ("sbuf", [128, 512], "uint8"),
+    "gb": ("sbuf", [128, 3, 512], "bfloat16"),
+    "mv": ("sbuf", [128, 3, 4, 32, 4], "bfloat16"),
+    "ysb": ("sbuf", [128, 1536], "float32"),
+    "pX": ("psum", [128, 1536], "float32"),
+    "pW": ("psum", [128, 1024], "float32"),
+    "pL": ("psum", [128, 512], "float32"),
+    "pY": ("psum", [128, 1024], "float32"),
+}
+for _b in ("xa", "xb", "xk", "wa", "wb", "wk"):
+    SCRATCH[_b] = ("sbuf", [128, 16], "int32")
+for _b in ("x1", "x2", "x3", "w1", "w2", "w3"):
+    SCRATCH[_b] = ("sbuf", [128, 16], "float32")
+for _l, _n in (("o", 4), ("a", 2)):
+    SCRATCH[_l + "u"] = ("sbuf", [128, 4, 8, 4], "float32")
+    SCRATCH[_l + "d"] = ("sbuf", [128, 8, 2, 16], "float32")
+    SCRATCH[_l + "z"] = ("sbuf", [128, 32, 8], "float32")
+    SCRATCH[_l + "off"] = ("sbuf", [128, 32 * _n], "uint16")
+for _k in range(2):
+    SCRATCH["xg%d" % _k] = ("sbuf", [128, 4 * XC], "bfloat16")
+for _b in range(3):
+    SCRATCH["gx%d" % _b] = ("sbuf", [128, 512], "float32")
+    SCRATCH["rq%d" % _b] = ("sbuf", [128, XC], "float8_e4m3fn_x4")
+    SCRATCH["rs%d" % _b] = ("sbuf", [128, XC], "uint8")
+for _k in range(4):
+    SCRATCH["gw%d" % _k] = ("sbuf", [128, 512], "float32")
+    SCRATCH["xt%d" % _k] = ("sbuf", [128, 3, 512] if _k == 2 else [128, 4 * XC], "bfloat16")
+    SCRATCH["xq%d" % _k] = ("sbuf", [128, XC], "float8_e4m3fn_x4")
+    SCRATCH["xs%d" % _k] = ("sbuf", [128, XC], "uint8")
+
+SEMAPHORES = (["V", "S", "P", "G", "sent", "lpk", "lxa", "lxb", "lw", "wsh", "xm"]
+              + ["xsh%d%d" % (c, q) for c in range(2) for q in range(2)]
+              + ["list%d" % k for k in range(3)] + ["arr%d" % k for k in range(3)]
+              + ["ig%d%d" % (k, t) for k in range(2) for t in range(4)]
+              + ["ys%d" % k for k in range(4)])
+
+
+def roles(core, T, topo):
+    me = T.rank_of(core)
+    far = [s for s in range(N) if topo.chip(T.cores[s]) != topo.chip(core)]
+    far.sort(key=lambda s: topo.die(T.cores[s]) != topo.die(core))
+    return far + [s for s in range(N) if s != me and s not in far]
+
+
+def rank_program(g, core, T, topo):
+    me = T.rank_of(core)
+    if me is None:
+        return
+    Q = {"V": g.vector, "S": g.scalar, "P": g.tensor, "G": g, "Y": g.sync}
+    count = {"V": 0, "S": 0, "P": 0, "G": 0}
+    seen = {}
+
+    def wait(q, *toks):
+        for name, val in toks:
+            if seen.get((q, name), 0) < val:
+                seen[(q, name)] = val
+                Q[q].wait_ge(T.sem[name], val)
+
+    def tick(q, ins):
+        count[q] += 1
+        ins.then_inc(T.sem[q], 1)
+        return (q, count[q])
+
+    def now(q):
+        return (q, count[q])
+
+    v, sc, pe, sy = g.vector, g.scalar, g.tensor, g.sync
+    D = roles(core, T, topo)
+    cores = T.cores
+    A = AluOpType
+
+    sc.dma_start(T.pk[:], T.pick[:]).then_inc(T.sem.lpk, 16)
+    sy.dma_start(T.nat[:, 0:24, :], T.x[0:1024, :]).then_inc(T.sem.lxa, 16)
+    sy.dma_start(T.nat[:, 24:48, :], T.x[1024:2048, :]).then_inc(T.sem.lxb, 16)
+    PK, LX, LW = ("lpk", 16), [("lxa", 16), ("lxb", 16)], ("lw", 16)
+
+    t_ones = tick("V", v.memset(T.ones[:], 1.0))
+    for l in "oa":
+        t_zero = tick("V", v.memset(T[l + "u"][:], 0.0))
+    wait("G", t_ones)
+    t_id = tick("G", g.affine_select(T.ident[:], T.ones[:], [[-1, 128]], A.is_equal, 0.0, 0, 1))
+
+    def shares(l, hi, lo, sh):
+        tick("V", v.tensor_scalar(T[l + "a"][:], T.pk[:], hi, None, A.bitwise_and))
+        tick("V", v.tensor_scalar(T[l + "b"][:], T.pk[:], lo, None, A.bitwise_and))
+        tick("V", v.tensor_scalar(T[l + "k"][:], T.pk[:], sh, 31, A.arith_shift_right, A.bitwise_and))
+
+    def scaled(l, s, mul):
+        tick("V", v.tensor_scalar(T[l + "1"][:], T[l + "a"][:], float(s), None, A.mult))
+        tick("V", v.tensor_scalar(T[l + "2"][:], T[l + "b"][:], float(mul), None, A.mult))
+
+    wait("V", PK)
+    shares("x", 0x700, 7, 3)
+    wait("V", now("V"))
+    scaled("x", 3, 96)
+    shares("w", 0x600, 15, 4)
+    wait("V", now("V"))
+    tick("V", v.tensor_tensor(T.x3[:], T.x1[:], T.x2[:], A.add))
+    scaled("w", 1, 32)
+    wait("V", now("V"))
+    t_fx = tick("V", v.tensor_tensor(T.fx[:], T.x3[:], T.xk[:], A.add))
+    tick("V", v.tensor_tensor(T.w3[:], T.w1[:], T.w2[:], A.add))
+    wait("V", now("V"))
+    t_fw = tick("V", v.tensor_tensor(T.fw[:], T.w3[:], T.wk[:], A.add))
+
+    eng = [topo.engines(core, cores[s]) for s in D]
+    picks = [eng[0][0:4], eng[1][4:8], eng[2][8:16]]
+
+    def transfer(k, src, dst):
+        rid, pid, _ = topo.addr(cores[D[k]])
+        return RemoteDMATransfer(dst_ids=[DstId(rid=rid, pnc=pid)], dma_engine_mask=sum(1 << e for e in picks[k]),
+                                 remote_sem=T.sem["list%d" % k], src=src, dst=dst)
+    wait("G", PK)
+    g.remote_dma_fused([transfer(0, T.pk[:, 4 * D[0]:4 * D[0] + 4], T.ld[:])], local_sem=T.sem.sent)
+    wait("G", t_fx)
+    g.remote_dma_fused([transfer(k, T.fx[:, 4 * D[k]:4 * D[k] + 4], T.la[:, k - 1, :]) for k in (1, 2)],
+                       local_sem=T.sem.sent)
+    LIST = [("list%d" % k, len(picks[k])) for k in range(3)]
+
+    def gather(k, idx, t):
+        g.indirect_dma_start(T["xg%d" % k][:, XC * t:XC * t + XC], None, T.x[:],
+                             IndirectOffsetOnAxis(ap=idx, axis=0), bounds_check=R - 1).then_inc(T.sem["ig%d%d" % (k, t)], 16)
+
+    def copy(q, out, in_):
+        if q == "V":
+            return tick("V", v.tensor_copy(out, in_))
+        return tick("S", sc.activation(out, in_, COPY))
+
+    def spread(l, n, src, toks):
+        done = []
+        for m in range(4):
+            q = "VS"[m % 2]
+            wait(q, t_zero, *toks)
+            done.append(copy(q, T[l + "u"][:, m, 0:n, :], src))
+        wait("P", t_id, *done)
+        tok = tick("P", pe.transpose(T.pL[:, 0:128], T[l + "u"][:], T.ident[:]))
+        wait("S", tok)
+        a = copy("S", T[l + "d"][:, :, 0, :], T.pL[:, 0:128])
+        wait("V", a)
+        b = copy("V", T[l + "d"][:, :, 1, :], T.pL[:, 0:128])
+        wait("V", b)
+        for k in range(8):
+            tick("V", v.transpose(T[l + "z"][:, :, k], T[l + "d"][:, k, :, :]))
+        wait("V", now("V"))
+        return tick("V", v.tensor_copy(T[l + "off"][:], T[l + "z"][:, 0:4 * n, :]))
+
+    def turn_x(c):
+        wait("V", LX[c])
+        toks = []
+        for q in range(4):
+            o = (4 * c + q) * XSLOT
+            toks.append(tick("V", v.transpose(T.stg[:, o:o + XSLOT], T.nat[:, 24 * c:24 * c + 24, 32 * q:32 * q + 32])))
+        for q in range(4):
+            for a in range(4):
+                d = a % 2
+                qq = ("Y", "S")[d]
+                wait(qq, toks[q])
+                Q[qq].dma_start(T.xw[32 * q:32 * q + 32, (4 * c + a) * XSLOT:(4 * c + a + 1) * XSLOT],
+                                T.stg[32 * a:32 * a + 32, (4 * c + q) * XSLOT:(4 * c + q + 1) * XSLOT]
+                                ).then_inc(T.sem["xsh%d%d" % (c, d)], 16)
+
+    t_offo = spread("o", 4, T.fw[:], [t_fw])
+    turn_x(0)
+    turn_x(1)
+    t_offa = spread("a", 2, T.la[:], LIST[1:3])
+    XSH = [("xsh%d%d" % (c, d), 128) for c in range(2) for d in range(2)]
+    WSH = ("wsh", 256)
+
+    def take(q, out, win, off):
+        if q == "V":
+            return tick("V", v.tensor_copy(out, win.indirect(off)))
+        return tick("S", sc.activation(out, win.indirect(off), COPY))
+
+    tok = {}
+    held = {}
+    place = {}
+    turn = {"pX": 0, "pW": 0, "pY": 0}
+    sums = {"sent": sum(len(e) for e in picks), "y": 0}
+
+    def bank(ps, n):
+        b = turn[ps] % n
+        turn[ps] += 1
+        return b
+
+    def turned(task, ps, n, buf):
+        b = bank(ps, n)
+        wait("P", t_id, tok["g" + task[1:]], *([tok[held[(ps, b)]]] if (ps, b) in held else []))
+        for t in range(4):
+            tick("P", pe.transpose(T[ps][:, 512 * b + t:512 * b + 512:4], buf[:, 128 * t:128 * t + 128], T.ident[:]))
+        held[(ps, b)] = "e" + task[1:]
+        tok[task] = now("P")
+        place[task] = b
+
+    def emptied(q, task, ps, out):
+        b = place["p" + task[1:]]
+        wait(q, tok["p" + task[1:]])
+        tok[task] = copy(q, out, T[ps][:, 512 * b:512 * b + 512])
+
+    def run(q, task):
+        kind, k, i = task[0], task[1], int(task[2:] or 0)
+        if task == "lw":
+            Q[q].dma_start(T.wn[:], T.w[:]).then_inc(T.sem.lw, 16)
+        elif task == "tw":
+            wait("V", LW)
+            for b in range(4):
+                tok[task] = tick("V", v.transpose(T.wst[:, b * WSLOT:b * WSLOT + WSLOT], T.wn[:, :, 32 * b:32 * b + 32]))
+        elif task == "cw":
+            wait(q, tok["tw"])
+            for b in range(4):
+                for a in range(4):
+                    Q[q].dma_start(T.ww[32 * b:32 * b + 32, a * WSLOT:(a + 1) * WSLOT],
+                                   T.wst[32 * a:32 * a + 32, b * WSLOT:(b + 1) * WSLOT]).then_inc(T.sem.wsh, 16)
+        elif kind == "g" and k == "w":
+            wait(q, t_offo, WSH)
+            tok[task] = take(q, T["gw%d" % i][:], T.ww[:], T.ooff[:, 32 * i:32 * i + 32])
+        elif kind == "g":
+            wait(q, t_offa, *XSH)
+            out = T["gx%d" % i][:] if k == "1" else T.gb[:, i, :]
+            tok[task] = take(q, out, T.xw[:, 32 * i:32 * i + XW - 64], T.aoff[:, 32 * int(k) - 32:32 * int(k)])
+        elif kind == "p" and k == "w":
+            turned(task, "pW", 2, T["gw%d" % i])
+        elif kind == "p":
+            turned(task, "pX", 3, T["gx%d" % i])
+        elif kind == "e" and k == "w":
+            emptied(q, task, "pW", T.wt[:, 512 * i:512 * i + 512])
+        elif kind == "e":
+            emptied(q, task, "pX", T.xt1[:, 512 * i:512 * i + 512])
+        elif task == "m2":
+            wait("V", *[tok["g2%d" % b] for b in range(3)])
+            for t in range(4):
+                tok[task] = tick("V", v.transpose(T.mv[:, :, :, :, t], T.gb[:, :, 128 * t:128 * t + 128]))
+        elif task == "d2":
+            wait(q, tok["m2"])
+            for a in range(4):
+                for b in range(4):
+                    Q[q].dma_start(T.xt2[32 * b:32 * b + 32, :, 128 * a:128 * a + 128],
+                                   T.mv[32 * a:32 * a + 32, :, b, :, :]).then_inc(T.sem.xm, 16)
+        elif kind == "l":
+            buf = "01"[k == "3"]
+            wait(q, ("ig%s%d" % (buf, i), 16))
+            tok[task] = copy(q, T["xt" + k][:, i:4 * XC:4], T["xg" + buf][:, XC * i:XC * i + XC])
+        elif task == "q2":
+            wait("V", ("xm", 256))
+            for b in range(3):
+                tok[task] = tick("V", v.quantize_mx(T.xq2[:, 128 * b:128 * b + 128], T.xs2[:, 128 * b:128 * b + 128],
+                                                    T.xt2[:, b, :]))
+        elif task == "qw":
+            wait("V", *[tok["ew%d" % b] for b in range(4)])
+            tok[task] = tick("V", v.quantize_mx(T.wq[:], T.ws[:], T.wt[:]))
+        elif kind == "q":
+            wait("V", *([tok["e1%d" % b] for b in range(3)] if k == "1" else [tok["l%s%d" % (k, t)] for t in range(4)]))
+            tok[task] = tick("V", v.quantize_mx(T["xq" + k][:], T["xs" + k][:], T["xt" + k][:]))
+        elif kind == "o":
+            t = int(k)
+            gather(1, T.pk[:, 4 * me + t:4 * me + t + 1], t)
+        elif kind == "i":
+            wait("G", LIST[0])
+            for t in range(4):
+                gather(0, T.ld[:, t:t + 1], t)
+        elif kind == "s":
+            c = cores[D[int(k)]]
+            rid, pid, _ = topo.addr(c)
+            wait("G", tok["q" + k])
+            g.remote_dma(T["rq" + k][:].bitcast(dt.uint8), T["xq" + k][:].bitcast(dt.uint8), T.sem["arr" + k], T.sem.sent,
+                         pid, rid, topo.mask(core, c))
+            g.remote_dma(T["rs" + k][:], T["xs" + k][:], T.sem["arr" + k], T.sem.sent, pid, rid, topo.mask(core, c))
+            sums["sent"] += 2 * len(eng[int(k)])
+        elif kind == "y":
+            s = (D + [me])[int(k)]
+            if k == "3":
+                xq, xs, arrived = T.xq3, T.xs3, tok["q3"]
+            else:
+                xq, xs, arrived = T["rq" + k], T["rs" + k], ("arr" + k, 2 * len(eng[int(k)]))
+            b = bank("pY", 2)
+            wait("P", tok["qw"], arrived, *([held[("pY", b)]] if ("pY", b) in held else []))
+            m = tick("P", pe.matmul_mx(T.pY[:, 512 * b:512 * b + XC], T.wq[:, 128 * s:128 * s + 128],
+                                       T.ws[:, 128 * s:128 * s + 128], xq[:], xs[:], True, True))
+            wait(q, m)
+            held[("pY", b)] = e = copy(q, T.ysb[:, XC * s:XC * s + XC], T.pY[:, 512 * b:512 * b + XC])
+            wait("Y", e)
+            sy.dma_start(T.y[:, XC * s:XC * s + XC], T.ysb[:, XC * s:XC * s + XC]).then_inc(T.sem["ys%d" % sums["y"]], 16)
+            sums["y"] += 1
+
+    for step in PLAN.split():
+        q, task = step.split(":")
+        run(q, task)
+    for i in range(4):
+        wait("Y", ("ys%d" % i, 16))
+    wait("Y", now("V"), now("S"), now("P"), now("G"))
+    wait("G", ("sent", sums["sent"]))

@@ -3,65 +3,68 @@ from concourse.mybir import dt, AluOpType, ActivationFunctionType
 
 N, R, XC = 4, 2048, 384
 COPY = ActivationFunctionType.Copy
-XW = 6144
-XSLOT = 768
-WSLOT = 512
+MODE = {1: "P", 2: "V"}
+CHUNKS = {"A": (0, 2), "B": (2, 4), "0": (0, 1), "1": (1, 2), "2": (2, 3), "3": (3, 4)}
 
 PLAN = """
-G:o1 G:i0 G:o0 G:o2
-Y:lw S:g12 P:p12 S:g20 V:g10 V:tw S:g22 V:g21 S:g11 P:p10 V:l00 P:p11 S:e10 V:m2 V:e11 S:l01 V:l02
-S:gw0 P:pw0 V:l03 S:gw1 V:q0 G:s0 V:ew0 V:e12 S:gw3 P:pw1 V:q1 P:pw3 S:l31 S:gw2 Y:cw S:l30 V:ew1 P:pw2
-Y:d2 V:ew3 V:q2 G:o3 S:l32 V:ew2 S:l33 V:qw S:y0 G:s1 V:q3 V:y3 V:y1 V:y2 G:s2
+Y:lx0 Y:lx1 Y:lx2 Y:lx3 Y:lw S:uo
+V:tx00 V:tx01 V:tx10 V:tx11 V:tx20 V:tx21 V:tx30 S:ax0 V:tx31 Y:ax1 V:txA2 V:txB2 Y:ax2 V:tw Y:aw
+G:o0 G:i0 G:i1 G:i2 G:i3 G:o1
+S:ua S:va V:za S:g120 V:g100 P:p10 S:g1a1 P:p11 S:g2a2 S:e10 S:gw1 V:g2a0 V:g2a1 V:g102 V:g122
+V:m20 V:m21 V:m22 Y:d2 V:e11 P:p12 V:e12 V:q1 G:s1 P:pw1 S:gw0 V:h0 V:l03 S:gw2 P:pw0 V:ew1 P:pw2
+S:gw3 S:l00 S:ew0 S:h1 P:pw3 V:q2 G:s2 V:l01 V:l02 V:q0 G:s0 V:l31 V:h2 V:ew2 V:qw1 S:ew3 V:qw3 V:qw2
+S:l30 P:p33 P:p32 V:e33 V:qw0 S:y1 S:y2 V:e32 V:q3 V:y3 S:y0
 """
 
 SCRATCH = {
     "ones": ("sbuf", [128, 128], "float32"),
     "ident": ("sbuf", [128, 128], "float32"),
-    "pk": ("sbuf", [128, 16], "int32"),
+    "pk": ("sbuf", [128, 24], "int32"),
     "ld": ("sbuf", [128, 4], "int32"),
-    "la": ("sbuf", [128, 2, 4], "float32"),
-    "fx": ("sbuf", [128, 16], "float32"),
+    "la": ("sbuf", [128, 8], "float32"),
+    "fx": ("sbuf", [128, 24], "float32"),
     "fw": ("sbuf", [128, 16], "float32"),
-    "nat": ("sbuf", [128, 48, 128], "bfloat16"),
-    "stg": ("sbuf", [128, XW], "bfloat16"),
-    "xw": ("sbuf", [128, XW], "bfloat16"),
-    "wn": ("sbuf", [128, 16, 128], "bfloat16"),
-    "wst": ("sbuf", [128, 2048], "bfloat16"),
+    "nat": ("sbuf", [128, 16, 3, 32, 4], "bfloat16"),
+    "stg": ("sbuf", [128, 4, 3, 512], "bfloat16"),
+    "wn": ("sbuf", [128, 16, 32, 4], "bfloat16"),
+    "wf": ("sbuf", [128, 2048], "float32"),
+    "wst": ("sbuf", [128, 4, 512], "bfloat16"),
     "ww": ("sbuf", [128, 2048], "bfloat16"),
     "wt": ("sbuf", [128, 2048], "bfloat16"),
     "wq": ("sbuf", [128, 512], "float8_e4m3fn_x4"),
     "ws": ("sbuf", [128, 512], "uint8"),
-    "gb": ("sbuf", [128, 3, 512], "bfloat16"),
-    "mv": ("sbuf", [128, 3, 4, 32, 4], "bfloat16"),
-    "ysb": ("sbuf", [128, 1536], "float32"),
+    "ysb": ("sbuf", [128, 4, 3, 4, 32], "float32"),
     "pX": ("psum", [128, 1536], "float32"),
     "pW": ("psum", [128, 1024], "float32"),
     "pL": ("psum", [128, 512], "float32"),
     "pY": ("psum", [128, 1024], "float32"),
 }
-for _b in ("xa", "xb", "xk", "wa", "wb", "wk"):
-    SCRATCH[_b] = ("sbuf", [128, 16], "int32")
-for _b in ("x1", "x2", "x3", "w1", "w2", "w3"):
-    SCRATCH[_b] = ("sbuf", [128, 16], "float32")
-for _l, _n in (("o", 4), ("a", 2)):
-    SCRATCH[_l + "u"] = ("sbuf", [128, 4, 8, 4], "float32")
-    SCRATCH[_l + "d"] = ("sbuf", [128, 8, 2, 16], "float32")
+for _l, _n in (("o", 5), ("a", 7)):
+    SCRATCH[_l + "u"] = ("sbuf", [128, 4, 32], "float32")
+    SCRATCH[_l + "v"] = ("sbuf", [128, 8, 2, 16], "float32")
     SCRATCH[_l + "z"] = ("sbuf", [128, 32, 8], "float32")
     SCRATCH[_l + "off"] = ("sbuf", [128, 32 * _n], "uint16")
+for _b in ("xa", "xb", "xk"):
+    SCRATCH[_b] = ("sbuf", [128, 24], "int32")
+for _b in ("x1", "x2", "x3"):
+    SCRATCH[_b] = ("sbuf", [128, 24], "float32")
 for _k in range(2):
     SCRATCH["xg%d" % _k] = ("sbuf", [128, 4 * XC], "bfloat16")
+    SCRATCH["gb%d" % (_k + 1)] = ("sbuf", [128, 3, 512], "bfloat16")
+    SCRATCH["mv%d" % (_k + 1)] = ("sbuf", [128, 4, 3, 32, 4], "bfloat16")
 for _b in range(3):
-    SCRATCH["gx%d" % _b] = ("sbuf", [128, 512], "float32")
+    SCRATCH["xw%d" % _b] = ("sbuf", [128, R], "bfloat16")
+    SCRATCH["gx%d" % (_b + 1)] = ("sbuf", [128, 3, 512], "float32")
     SCRATCH["rq%d" % _b] = ("sbuf", [128, XC], "float8_e4m3fn_x4")
     SCRATCH["rs%d" % _b] = ("sbuf", [128, XC], "uint8")
 for _k in range(4):
     SCRATCH["gw%d" % _k] = ("sbuf", [128, 512], "float32")
-    SCRATCH["xt%d" % _k] = ("sbuf", [128, 3, 512] if _k == 2 else [128, 4 * XC], "bfloat16")
+    SCRATCH["xt%d" % _k] = ("sbuf", [128, 4 * XC], "bfloat16")
     SCRATCH["xq%d" % _k] = ("sbuf", [128, XC], "float8_e4m3fn_x4")
     SCRATCH["xs%d" % _k] = ("sbuf", [128, XC], "uint8")
 
-SEMAPHORES = (["V", "S", "P", "G", "sent", "lpk", "lxa", "lxb", "lw", "wsh", "xm"]
-              + ["xsh%d%d" % (c, q) for c in range(2) for q in range(2)]
+SEMAPHORES = (["V", "S", "P", "G", "sent", "lpk", "lpj", "lw", "wsh"]
+              + ["lx%d" % c for c in range(4)] + ["xsh%d" % b for b in range(3)] + ["xm%d" % k for k in (1, 2)]
               + ["list%d" % k for k in range(3)] + ["arr%d" % k for k in range(3)]
               + ["ig%d%d" % (k, t) for k in range(2) for t in range(4)]
               + ["ys%d" % k for k in range(4)])
@@ -98,54 +101,62 @@ def rank_program(g, core, T, topo):
 
     v, sc, pe, sy = g.vector, g.scalar, g.tensor, g.sync
     D = roles(core, T, topo)
+    DM = D + [me]
     cores = T.cores
     A = AluOpType
+    steps = [s.split(":") for s in PLAN.split()]
+    names = [t for q, t in steps]
+    own = len([t for t in names if t[0] == "o"])
+    merged, wpe = "zo" not in names, "cw0" in names
 
-    sc.dma_start(T.pk[:], T.pick[:]).then_inc(T.sem.lpk, 16)
-    sy.dma_start(T.nat[:, 0:24, :], T.x[0:1024, :]).then_inc(T.sem.lxa, 16)
-    sy.dma_start(T.nat[:, 24:48, :], T.x[1024:2048, :]).then_inc(T.sem.lxb, 16)
-    PK, LX, LW = ("lpk", 16), [("lxa", 16), ("lxb", 16)], ("lw", 16)
+    sc.dma_start(T.pk[:, 0:16], T.pick[:]).then_inc(T.sem.lpk, 16)
+    col = {}
+    nj = 0
+    for k in (1, 2):
+        col[k] = 4 * D[k]
+        if MODE[k] == "V":
+            col[k] = 16 + 4 * nj
+            nj += 1
+            for s in range(4):
+                sy.dma_start(T.pk[32 * s:32 * s + 32, col[k]:col[k] + 4], T.pick[s:128:4, 4 * D[k]:4 * D[k] + 4]
+                             ).then_inc(T.sem.lpj, 16)
+    PK, PJ, LW = ("lpk", 16), ("lpj", 64 * nj), ("lw", 16 if wpe else 64)
+    NX = 16 + 4 * nj
 
     t_ones = tick("V", v.memset(T.ones[:], 1.0))
-    for l in "oa":
+    for l in "a" if merged else "oa":
         t_zero = tick("V", v.memset(T[l + "u"][:], 0.0))
     wait("G", t_ones)
     t_id = tick("G", g.affine_select(T.ident[:], T.ones[:], [[-1, 128]], A.is_equal, 0.0, 0, 1))
 
-    def shares(l, hi, lo, sh):
-        tick("V", v.tensor_scalar(T[l + "a"][:], T.pk[:], hi, None, A.bitwise_and))
-        tick("V", v.tensor_scalar(T[l + "b"][:], T.pk[:], lo, None, A.bitwise_and))
-        tick("V", v.tensor_scalar(T[l + "k"][:], T.pk[:], sh, 31, A.arith_shift_right, A.bitwise_and))
-
-    def scaled(l, s, mul):
-        tick("V", v.tensor_scalar(T[l + "1"][:], T[l + "a"][:], float(s), None, A.mult))
-        tick("V", v.tensor_scalar(T[l + "2"][:], T[l + "b"][:], float(mul), None, A.mult))
-
-    wait("V", PK)
-    shares("x", 0x700, 7, 3)
+    wait("V", PK, PJ)
+    tick("V", v.tensor_scalar(T.xa[:, 0:NX], T.pk[:, 0:NX], 0x180, None, A.bitwise_and))
+    tick("V", v.tensor_scalar(T.xb[:, 0:NX], T.pk[:, 0:NX], 3, None, A.bitwise_and))
+    tick("V", v.tensor_scalar(T.xk[:, 0:NX], T.pk[:, 0:NX], 2, 0x19F, A.arith_shift_right, A.bitwise_and))
     wait("V", now("V"))
-    scaled("x", 3, 96)
-    shares("w", 0x600, 15, 4)
+    tick("V", v.tensor_scalar(T.x1[:, 0:NX], T.xa[:, 0:NX], 4.0, None, A.mult))
+    tick("V", v.tensor_scalar(T.x2[:, 0:NX], T.xb[:, 0:NX], 32.0, None, A.mult))
     wait("V", now("V"))
-    tick("V", v.tensor_tensor(T.x3[:], T.x1[:], T.x2[:], A.add))
-    scaled("w", 1, 32)
+    tick("V", v.tensor_tensor(T.x3[:, 0:NX], T.x1[:, 0:NX], T.x2[:, 0:NX], A.add))
     wait("V", now("V"))
-    t_fx = tick("V", v.tensor_tensor(T.fx[:], T.x3[:], T.xk[:], A.add))
-    tick("V", v.tensor_tensor(T.w3[:], T.w1[:], T.w2[:], A.add))
-    wait("V", now("V"))
-    t_fw = tick("V", v.tensor_tensor(T.fw[:], T.w3[:], T.wk[:], A.add))
+    t_fx = tick("V", v.tensor_tensor(T.fx[:, 0:NX], T.x3[:, 0:NX], T.xk[:, 0:NX], A.add))
 
     eng = [topo.engines(core, cores[s]) for s in D]
-    picks = [eng[0][0:4], eng[1][4:8], eng[2][8:16]]
+    far = len(eng[0])
+    picks = [eng[0][:far // 2], eng[1][far // 2:], [e for e in eng[2] if e not in eng[0]]]
+    lanes = [eng[0], eng[1], picks[2]]
+
+    def mask(es):
+        return sum(1 << e for e in es)
 
     def transfer(k, src, dst):
         rid, pid, _ = topo.addr(cores[D[k]])
-        return RemoteDMATransfer(dst_ids=[DstId(rid=rid, pnc=pid)], dma_engine_mask=sum(1 << e for e in picks[k]),
+        return RemoteDMATransfer(dst_ids=[DstId(rid=rid, pnc=pid)], dma_engine_mask=mask(picks[k]),
                                  remote_sem=T.sem["list%d" % k], src=src, dst=dst)
     wait("G", PK)
     g.remote_dma_fused([transfer(0, T.pk[:, 4 * D[0]:4 * D[0] + 4], T.ld[:])], local_sem=T.sem.sent)
     wait("G", t_fx)
-    g.remote_dma_fused([transfer(k, T.fx[:, 4 * D[k]:4 * D[k] + 4], T.la[:, k - 1, :]) for k in (1, 2)],
+    g.remote_dma_fused([transfer(k, T.fx[:, col[k]:col[k] + 4], T.la[:, 4 * k - 4:4 * k]) for k in (1, 2)],
                        local_sem=T.sem.sent)
     LIST = [("list%d" % k, len(picks[k])) for k in range(3)]
 
@@ -158,165 +169,221 @@ def rank_program(g, core, T, topo):
             return tick("V", v.tensor_copy(out, in_))
         return tick("S", sc.activation(out, in_, COPY))
 
-    def spread(l, n, src, toks):
-        done = []
-        for m in range(4):
-            q = "VS"[m % 2]
-            wait(q, t_zero, *toks)
-            done.append(copy(q, T[l + "u"][:, m, 0:n, :], src))
-        wait("P", t_id, *done)
-        tok = tick("P", pe.transpose(T.pL[:, 0:128], T[l + "u"][:], T.ident[:]))
-        wait("S", tok)
-        a = copy("S", T[l + "d"][:, :, 0, :], T.pL[:, 0:128])
-        wait("V", a)
-        b = copy("V", T[l + "d"][:, :, 1, :], T.pL[:, 0:128])
-        wait("V", b)
-        for k in range(8):
-            tick("V", v.transpose(T[l + "z"][:, :, k], T[l + "d"][:, k, :, :]))
-        wait("V", now("V"))
-        return tick("V", v.tensor_copy(T[l + "off"][:], T[l + "z"][:, 0:4 * n, :]))
-
-    def turn_x(c):
-        wait("V", LX[c])
-        toks = []
-        for q in range(4):
-            o = (4 * c + q) * XSLOT
-            toks.append(tick("V", v.transpose(T.stg[:, o:o + XSLOT], T.nat[:, 24 * c:24 * c + 24, 32 * q:32 * q + 32])))
-        for q in range(4):
-            for a in range(4):
-                d = a % 2
-                qq = ("Y", "S")[d]
-                wait(qq, toks[q])
-                Q[qq].dma_start(T.xw[32 * q:32 * q + 32, (4 * c + a) * XSLOT:(4 * c + a + 1) * XSLOT],
-                                T.stg[32 * a:32 * a + 32, (4 * c + q) * XSLOT:(4 * c + q + 1) * XSLOT]
-                                ).then_inc(T.sem["xsh%d%d" % (c, d)], 16)
-
-    t_offo = spread("o", 4, T.fw[:], [t_fw])
-    turn_x(0)
-    turn_x(1)
-    t_offa = spread("a", 2, T.la[:], LIST[1:3])
-    XSH = [("xsh%d%d" % (c, d), 128) for c in range(2) for d in range(2)]
-    WSH = ("wsh", 256)
-
     def take(q, out, win, off):
         if q == "V":
             return tick("V", v.tensor_copy(out, win.indirect(off)))
         return tick("S", sc.activation(out, win.indirect(off), COPY))
 
+    ob, o0 = ("a", 8) if merged else ("o", 0)
+    ox = 8 * (o0 + 16) if wpe else 8 * (o0 + 4 * me)
     tok = {}
-    held = {}
-    place = {}
+    ysum = [0]
+    sent = [sum(len(e) for e in picks)]
+    WSH = ("wsh", 64)
     turn = {"pX": 0, "pW": 0, "pY": 0}
-    sums = {"sent": sum(len(e) for e in picks), "y": 0}
+    held, place = {}, {}
+    calls = {k: 2 + len([t for t in names if t[:2] == "r" + k]) for k in "012"}
+    gone = {k: 0 for k in "012"}
 
-    def bank(ps, n):
-        b = turn[ps] % n
+    def done(prefix, last=""):
+        return [tok[t] for t in names if t.startswith(prefix) and t.endswith(last)]
+
+    def gathered(k, t, b):
+        return tok.get("g%sa%d" % (k, b)) or tok["g%s%d%d" % (k, t & 2, b)]
+
+    def bank(ps, reader):
+        b = turn[ps] % (T[ps].shape[1] // 512)
         turn[ps] += 1
-        return b
+        if (ps, b) in held:
+            wait("P", tok[held[(ps, b)]])
+        held[(ps, b)] = reader
+        place[reader] = 512 * b
+        return 512 * b
 
-    def turned(task, ps, n, buf):
-        b = bank(ps, n)
-        wait("P", t_id, tok["g" + task[1:]], *([tok[held[(ps, b)]]] if (ps, b) in held else []))
-        for t in range(4):
-            tick("P", pe.transpose(T[ps][:, 512 * b + t:512 * b + 512:4], buf[:, 128 * t:128 * t + 128], T.ident[:]))
-        held[(ps, b)] = "e" + task[1:]
-        tok[task] = now("P")
-        place[task] = b
-
-    def emptied(q, task, ps, out):
-        b = place["p" + task[1:]]
-        wait(q, tok["p" + task[1:]])
-        tok[task] = copy(q, out, T[ps][:, 512 * b:512 * b + 512])
+    def send(k, name, a, b):
+        rid, pid, _ = topo.addr(cores[D[int(k)]])
+        out, in_ = T["r" + name + k][:, a:b], T["x" + name + k][:, a:b]
+        if name == "q":
+            out, in_ = out.bitcast(dt.uint8), in_.bitcast(dt.uint8)
+        g.remote_dma(out, in_, T.sem["arr" + k], T.sem.sent, pid, rid, mask(lanes[int(k)]))
+        sent[0] += len(lanes[int(k)])
 
     def run(q, task):
-        kind, k, i = task[0], task[1], int(task[2:] or 0)
-        if task == "lw":
+        kind, k = task[0], task[1]
+        i = int(task[-1]) if len(task) > 2 else 0
+        if task[:2] == "lx":
+            Q[q].dma_start(T.nat[:, 4 * i:4 * i + 4], T.x[512 * i:512 * i + 512, :]).then_inc(T.sem[task], 16)
+        elif task[:2] == "tx":
+            c, e = CHUNKS[task[2]]
+            wait("V", *[("lx%d" % z, 16) for z in range(c, e)])
+            for s in range(4):
+                tok[task] = tick("V", v.transpose(T.stg[:, s, i, 128 * c:128 * e], T.nat[:, 4 * c:4 * e, i, :, s]))
+        elif task[:2] == "ax":
+            wait(q, *done("tx", task[2]))
+            for a in range(4):
+                Q[q].dma_start(T["xw%d" % i][:, 512 * a:512 * a + 512], T.stg[32 * a:32 * a + 32, :, i, :]
+                               ).then_inc(T.sem["xsh%d" % i], 16)
+        elif task == "lw" and wpe:
             Q[q].dma_start(T.wn[:], T.w[:]).then_inc(T.sem.lw, 16)
+        elif task == "lw":
+            for c in range(4):
+                Q[q].dma_start(T.wn[:, 4 * c:4 * c + 4], T.w[512 * c:512 * c + 512, :]).then_inc(T.sem.lw, 16)
+        elif task[:2] == "cw":
+            wait(q, LW)
+            tok[task] = copy(q, T.wf[:, 512 * i:512 * i + 512], T.wn[:, 4 * i:4 * i + 4])
+        elif task[:2] == "tw" and wpe:
+            wait("P", t_id, tok["cw%d" % i])
+            b = bank("pW", "fw%d" % i)
+            for t in range(4):
+                o = 512 * i + 128 * t
+                tok[task] = tick("P", pe.transpose(T.pW[:, b + 128 * t:b + 128 * t + 128], T.wf[:, o:o + 128], T.ident[:]))
+        elif task[:2] == "fw":
+            wait(q, tok["tw%d" % i])
+            tok[task] = copy(q, T.ww[:, 512 * i:512 * i + 512], T.pW[:, place[task]:place[task] + 512])
+        elif task == "pw":
+            wait("V", t_fx)
+            tick("V", v.tensor_scalar(T.xa[:, 0:16], T.pk[:, 0:16], 15, None, A.bitwise_and))
+            tick("V", v.tensor_scalar(T.xk[:, 0:16], T.pk[:, 0:16], 4, None, A.arith_shift_right))
+            wait("V", now("V"))
+            tick("V", v.tensor_scalar(T.x1[:, 0:16], T.xa[:, 0:16], 128.0, None, A.mult))
+            wait("V", now("V"))
+            tok[task] = tick("V", v.tensor_tensor(T.fw[:], T.x1[:, 0:16], T.xk[:, 0:16], A.add))
         elif task == "tw":
             wait("V", LW)
             for b in range(4):
-                tok[task] = tick("V", v.transpose(T.wst[:, b * WSLOT:b * WSLOT + WSLOT], T.wn[:, :, 32 * b:32 * b + 32]))
-        elif task == "cw":
+                tok[task] = tick("V", v.transpose(T.wst[:, b, :], T.wn[:, :, :, b]))
+        elif task == "aw":
             wait(q, tok["tw"])
-            for b in range(4):
-                for a in range(4):
-                    Q[q].dma_start(T.ww[32 * b:32 * b + 32, a * WSLOT:(a + 1) * WSLOT],
-                                   T.wst[32 * a:32 * a + 32, b * WSLOT:(b + 1) * WSLOT]).then_inc(T.sem.wsh, 16)
-        elif kind == "g" and k == "w":
-            wait(q, t_offo, WSH)
-            tok[task] = take(q, T["gw%d" % i][:], T.ww[:], T.ooff[:, 32 * i:32 * i + 32])
-        elif kind == "g":
-            wait(q, t_offa, *XSH)
-            out = T["gx%d" % i][:] if k == "1" else T.gb[:, i, :]
-            tok[task] = take(q, out, T.xw[:, 32 * i:32 * i + XW - 64], T.aoff[:, 32 * int(k) - 32:32 * int(k)])
-        elif kind == "p" and k == "w":
-            turned(task, "pW", 2, T["gw%d" % i])
-        elif kind == "p":
-            turned(task, "pX", 3, T["gx%d" % i])
-        elif kind == "e" and k == "w":
-            emptied(q, task, "pW", T.wt[:, 512 * i:512 * i + 512])
-        elif kind == "e":
-            emptied(q, task, "pX", T.xt1[:, 512 * i:512 * i + 512])
-        elif task == "m2":
-            wait("V", *[tok["g2%d" % b] for b in range(3)])
-            for t in range(4):
-                tok[task] = tick("V", v.transpose(T.mv[:, :, :, :, t], T.gb[:, :, 128 * t:128 * t + 128]))
-        elif task == "d2":
-            wait(q, tok["m2"])
             for a in range(4):
-                for b in range(4):
-                    Q[q].dma_start(T.xt2[32 * b:32 * b + 32, :, 128 * a:128 * a + 128],
-                                   T.mv[32 * a:32 * a + 32, :, b, :, :]).then_inc(T.sem.xm, 16)
+                Q[q].dma_start(T.ww[:, 512 * a:512 * a + 512], T.wst[32 * a:32 * a + 32]).then_inc(T.sem.wsh, 16)
+        elif kind == "u":
+            wait(q, t_zero, *(LIST[1:3] if k == "a" else [tok["pw"] if wpe else t_fx]))
+            for m in range(4):
+                if k == "a":
+                    t = copy(q, T.au[:, m, 0:8], T.la[:])
+                else:
+                    t = copy(q, T[ob + "u"][:, m, o0:o0 + 16], T.fw[:] if wpe else T.fx[:, 0:16])
+                    if wpe and own < 4:
+                        t = copy(q, T[ob + "u"][:, m, o0 + 16:o0 + 20], T.fx[:, 4 * me:4 * me + 4])
+            if k == "o" and merged:
+                tok["uo"] = tok["vo"] = t
+            else:
+                wait("P", t_id, t, *[tok["v" + u[1]] for u in tok if u[0] == "u"])
+                tok[task] = tick("P", pe.transpose(T.pL[:, 0:128], T[k + "u"][:], T.ident[:]))
+        elif kind == "v":
+            wait(q, tok["u" + k])
+            for d in range(2):
+                tok[task] = copy(q, T[k + "v"][:, :, d, :], T.pL[:, 0:128])
+        elif kind == "z":
+            wait("V", tok["v" + k])
+            for u in range(8):
+                tick("V", v.transpose(T[k + "z"][:, :, u], T[k + "v"][:, u, :, :]))
+            wait("V", now("V"))
+            n = 8 if k == "a" and not merged else o0 + 16 + 4 * wpe
+            tok[task] = tick("V", v.tensor_copy(T[k + "off"][:, 0:8 * n], T[k + "z"][:, 0:n, :]))
+            if merged:
+                tok["zo"] = tok[task]
+        elif kind == "g" and k == "w":
+            o = 8 * o0 + 32 * DM[i]
+            wait(q, tok["zo"], *(done("fw") if wpe else [WSH]))
+            tok[task] = take(q, T["gw%d" % i][:], T.ww[:], T[ob + "off"][:, o:o + 32])
+        elif kind == "g":
+            t, e = (0, 4) if task[2] == "a" else (int(task[2]), int(task[2]) + 2)
+            o = 32 * int(k) - 32
+            wait(q, tok["za"], ("xsh%d" % i, 64))
+            out = T[("gb" if MODE[int(k)] == "V" else "gx") + k][:, i, 128 * t:128 * e]
+            tok[task] = take(q, out, T["xw%d" % i][:], T.aoff[:, o + 8 * t:o + 8 * e])
+        elif kind == "h":
+            wait(q, tok["zo"], ("xsh" + k, 64))
+            tok[task] = take(q, T.gx3[:, int(k), 128 * own:512], T["xw" + k][:], T[ob + "off"][:, ox + 8 * own:ox + 32])
+        elif kind == "m":
+            for t in range(4):
+                wait("V", gathered(k, t, i))
+                tok[task] = tick("V", v.transpose(T["mv" + k][:, :, i, :, t], T["gb" + k][:, i, 128 * t:128 * t + 128]))
+        elif kind == "d":
+            wait(q, *done("m" + k))
+            for a in range(4):
+                Q[q].dma_start(T["xt" + k][:, XC * a:XC * a + XC], T["mv" + k][32 * a:32 * a + 32]
+                               ).then_inc(T.sem["xm" + k], 16)
+        elif kind == "p" and k == "w":
+            wait("P", t_id, tok["gw%d" % i])
+            b = bank("pW", "ew%d" % i)
+            for t in range(4):
+                tok[task] = tick("P", pe.transpose(T.pW[:, b + t:b + 512:4], T["gw%d" % i][:, 128 * t:128 * t + 128], T.ident[:]))
+        elif kind == "p" and k == "3":
+            wait("P", t_id, *done("h"))
+            o = bank("pX", "e3%d" % i)
+            for b in range(3):
+                tok[task] = tick("P", pe.transpose(T.pX[:, o + 128 * b:o + 128 * b + 128],
+                                                   T.gx3[:, b, 128 * i:128 * i + 128], T.ident[:]))
+        elif kind == "p":
+            wait("P", t_id, gathered(k, 0, i))
+            b = bank("pX", "e%s%d" % (k, i))
+            for t in range(4):
+                wait("P", gathered(k, t, i))
+                tok[task] = tick("P", pe.transpose(T.pX[:, b + t:b + 512:4], T["gx" + k][:, i, 128 * t:128 * t + 128], T.ident[:]))
+        elif kind == "e" and k == "w":
+            wait(q, tok["pw%d" % i])
+            tok[task] = copy(q, T.wt[:, 512 * i:512 * i + 512], T.pW[:, place[task]:place[task] + 512])
+        elif kind == "e" and k == "3":
+            wait(q, tok["p3%d" % i])
+            tok[task] = copy(q, T.xt3[:, i:4 * XC:4], T.pX[:, place[task]:place[task] + XC])
+        elif kind == "e":
+            wait(q, tok["p%s%d" % (k, i)])
+            tok[task] = copy(q, T["xt" + k][:, 512 * i:512 * i + 512], T.pX[:, place[task]:place[task] + 512])
         elif kind == "l":
             buf = "01"[k == "3"]
             wait(q, ("ig%s%d" % (buf, i), 16))
             tok[task] = copy(q, T["xt" + k][:, i:4 * XC:4], T["xg" + buf][:, XC * i:XC * i + XC])
-        elif task == "q2":
-            wait("V", ("xm", 256))
-            for b in range(3):
-                tok[task] = tick("V", v.quantize_mx(T.xq2[:, 128 * b:128 * b + 128], T.xs2[:, 128 * b:128 * b + 128],
-                                                    T.xt2[:, b, :]))
         elif task == "qw":
-            wait("V", *[tok["ew%d" % b] for b in range(4)])
+            wait("V", *done("ew"))
             tok[task] = tick("V", v.quantize_mx(T.wq[:], T.ws[:], T.wt[:]))
+        elif kind == "q" and len(task) == 3:
+            n = {"w": "w%s", "1": "x%s1", "2": "x%s2"}[k]
+            wait("V", tok["e" + task[1:]])
+            tok[task] = tick("V", v.quantize_mx(T[n % "q"][:, 128 * i:128 * i + 128], T[n % "s"][:, 128 * i:128 * i + 128],
+                                                T[n % "t"][:, 512 * i:512 * i + 512]))
         elif kind == "q":
-            wait("V", *([tok["e1%d" % b] for b in range(3)] if k == "1" else [tok["l%s%d" % (k, t)] for t in range(4)]))
+            wait("V", *([("xm" + k, 64)] if MODE.get(int(k)) == "V" else done("l" + k) + done("e" + k)))
             tok[task] = tick("V", v.quantize_mx(T["xq" + k][:], T["xs" + k][:], T["xt" + k][:]))
         elif kind == "o":
             t = int(k)
             gather(1, T.pk[:, 4 * me + t:4 * me + t + 1], t)
         elif kind == "i":
             wait("G", LIST[0])
-            for t in range(4):
-                gather(0, T.ld[:, t:t + 1], t)
+            gather(0, T.ld[:, int(k):int(k) + 1], int(k))
+        elif kind == "r":
+            wait("G", *[tok["q%s%d" % (k, b)] for b in range(i + 1)])
+            send(k, "q", gone[k], 128 * i + 128)
+            gone[k] = 128 * i + 128
         elif kind == "s":
-            c = cores[D[int(k)]]
-            rid, pid, _ = topo.addr(c)
-            wait("G", tok["q" + k])
-            g.remote_dma(T["rq" + k][:].bitcast(dt.uint8), T["xq" + k][:].bitcast(dt.uint8), T.sem["arr" + k], T.sem.sent,
-                         pid, rid, topo.mask(core, c))
-            g.remote_dma(T["rs" + k][:], T["xs" + k][:], T.sem["arr" + k], T.sem.sent, pid, rid, topo.mask(core, c))
-            sums["sent"] += 2 * len(eng[int(k)])
+            wait("G", *done("q" + k))
+            send(k, "q", gone[k], XC)
+            send(k, "s", 0, XC)
         elif kind == "y":
-            s = (D + [me])[int(k)]
+            j = int(k)
+            s = DM[j]
             if k == "3":
                 xq, xs, arrived = T.xq3, T.xs3, tok["q3"]
             else:
-                xq, xs, arrived = T["rq" + k], T["rs" + k], ("arr" + k, 2 * len(eng[int(k)]))
-            b = bank("pY", 2)
-            wait("P", tok["qw"], arrived, *([held[("pY", b)]] if ("pY", b) in held else []))
-            m = tick("P", pe.matmul_mx(T.pY[:, 512 * b:512 * b + XC], T.wq[:, 128 * s:128 * s + 128],
-                                       T.ws[:, 128 * s:128 * s + 128], xq[:], xs[:], True, True))
+                xq, xs, arrived = T["rq" + k], T["rs" + k], ("arr" + k, calls[k] * len(lanes[j]))
+            wait("P", tok["qw"] if "qw" in tok else tok["qw" + k], arrived)
+            b = bank("pY", task)
+            m = tick("P", pe.matmul_mx(T.pY[:, b:b + XC], T.wq[:, 128 * j:128 * j + 128],
+                                       T.ws[:, 128 * j:128 * j + 128], xq[:], xs[:], True, True))
             wait(q, m)
-            held[("pY", b)] = e = copy(q, T.ysb[:, XC * s:XC * s + XC], T.pY[:, 512 * b:512 * b + XC])
-            wait("Y", e)
-            sy.dma_start(T.y[:, XC * s:XC * s + XC], T.ysb[:, XC * s:XC * s + XC]).then_inc(T.sem["ys%d" % sums["y"]], 16)
-            sums["y"] += 1
+            if MODE.get(j) != "V":
+                tok[task] = copy(q, T.ysb[:, s], T.pY[:, b:b + XC])
+            else:
+                for a in range(4):
+                    tok[task] = copy(q, T.ysb[:, s, :, a, :], T.pY[:, b + 96 * a:b + 96 * a + 96])
+            wait("Y", tok[task])
+            sy.dma_start(T.y[:, XC * s:XC * s + XC], T.ysb[:, s]).then_inc(T.sem["ys%d" % ysum[0]], 16)
+            ysum[0] += 1
 
-    for step in PLAN.split():
-        q, task = step.split(":")
+    for q, task in steps:
         run(q, task)
     for i in range(4):
         wait("Y", ("ys%d" % i, 16))
     wait("Y", now("V"), now("S"), now("P"), now("G"))
-    wait("G", ("sent", sums["sent"]))
+    wait("G", ("sent", sent[0]))

from concourse.bass import DstId, IndirectOffsetOnAxis, RemoteDMATransfer
from concourse.mybir import dt, AluOpType, ActivationFunctionType

N, R, XC = 4, 2048, 384
COPY = ActivationFunctionType.Copy
MODE = {1: "P", 2: "V"}
CHUNKS = {"A": (0, 2), "B": (2, 4), "0": (0, 1), "1": (1, 2), "2": (2, 3), "3": (3, 4)}

PLAN = """
Y:lx0 Y:lx1 Y:lx2 Y:lx3 Y:lw S:uo
V:tx00 V:tx01 V:tx10 V:tx11 V:tx20 V:tx21 V:tx30 S:ax0 V:tx31 Y:ax1 V:txA2 V:txB2 Y:ax2 V:tw Y:aw
G:o0 G:i0 G:i1 G:i2 G:i3 G:o1
S:ua S:va V:za S:g120 V:g100 P:p10 S:g1a1 P:p11 S:g2a2 S:e10 S:gw1 V:g2a0 V:g2a1 V:g102 V:g122
V:m20 V:m21 V:m22 Y:d2 V:e11 P:p12 V:e12 V:q1 G:s1 P:pw1 S:gw0 V:h0 V:l03 S:gw2 P:pw0 V:ew1 P:pw2
S:gw3 S:l00 S:ew0 S:h1 P:pw3 V:q2 G:s2 V:l01 V:l02 V:q0 G:s0 V:l31 V:h2 V:ew2 V:qw1 S:ew3 V:qw3 V:qw2
S:l30 P:p33 P:p32 V:e33 V:qw0 S:y1 S:y2 V:e32 V:q3 V:y3 S:y0
"""

SCRATCH = {
    "ones": ("sbuf", [128, 128], "float32"),
    "ident": ("sbuf", [128, 128], "float32"),
    "pk": ("sbuf", [128, 24], "int32"),
    "ld": ("sbuf", [128, 4], "int32"),
    "la": ("sbuf", [128, 8], "float32"),
    "fx": ("sbuf", [128, 24], "float32"),
    "fw": ("sbuf", [128, 16], "float32"),
    "nat": ("sbuf", [128, 16, 3, 32, 4], "bfloat16"),
    "stg": ("sbuf", [128, 4, 3, 512], "bfloat16"),
    "wn": ("sbuf", [128, 16, 32, 4], "bfloat16"),
    "wf": ("sbuf", [128, 2048], "float32"),
    "wst": ("sbuf", [128, 4, 512], "bfloat16"),
    "ww": ("sbuf", [128, 2048], "bfloat16"),
    "wt": ("sbuf", [128, 2048], "bfloat16"),
    "wq": ("sbuf", [128, 512], "float8_e4m3fn_x4"),
    "ws": ("sbuf", [128, 512], "uint8"),
    "ysb": ("sbuf", [128, 4, 3, 4, 32], "float32"),
    "pX": ("psum", [128, 1536], "float32"),
    "pW": ("psum", [128, 1024], "float32"),
    "pL": ("psum", [128, 512], "float32"),
    "pY": ("psum", [128, 1024], "float32"),
}
for _l, _n in (("o", 5), ("a", 7)):
    SCRATCH[_l + "u"] = ("sbuf", [128, 4, 32], "float32")
    SCRATCH[_l + "v"] = ("sbuf", [128, 8, 2, 16], "float32")
    SCRATCH[_l + "z"] = ("sbuf", [128, 32, 8], "float32")
    SCRATCH[_l + "off"] = ("sbuf", [128, 32 * _n], "uint16")
for _b in ("xa", "xb", "xk"):
    SCRATCH[_b] = ("sbuf", [128, 24], "int32")
for _b in ("x1", "x2", "x3"):
    SCRATCH[_b] = ("sbuf", [128, 24], "float32")
for _k in range(2):
    SCRATCH["xg%d" % _k] = ("sbuf", [128, 4 * XC], "bfloat16")
    SCRATCH["gb%d" % (_k + 1)] = ("sbuf", [128, 3, 512], "bfloat16")
    SCRATCH["mv%d" % (_k + 1)] = ("sbuf", [128, 4, 3, 32, 4], "bfloat16")
for _b in range(3):
    SCRATCH["xw%d" % _b] = ("sbuf", [128, R], "bfloat16")
    SCRATCH["gx%d" % (_b + 1)] = ("sbuf", [128, 3, 512], "float32")
    SCRATCH["rq%d" % _b] = ("sbuf", [128, XC], "float8_e4m3fn_x4")
    SCRATCH["rs%d" % _b] = ("sbuf", [128, XC], "uint8")
for _k in range(4):
    SCRATCH["gw%d" % _k] = ("sbuf", [128, 512], "float32")
    SCRATCH["xt%d" % _k] = ("sbuf", [128, 4 * XC], "bfloat16")
    SCRATCH["xq%d" % _k] = ("sbuf", [128, XC], "float8_e4m3fn_x4")
    SCRATCH["xs%d" % _k] = ("sbuf", [128, XC], "uint8")

SEMAPHORES = (["V", "S", "P", "G", "sent", "lpk", "lpj", "lw", "wsh"]
              + ["lx%d" % c for c in range(4)] + ["xsh%d" % b for b in range(3)] + ["xm%d" % k for k in (1, 2)]
              + ["list%d" % k for k in range(3)] + ["arr%d" % k for k in range(3)]
              + ["ig%d%d" % (k, t) for k in range(2) for t in range(4)]
              + ["ys%d" % k for k in range(4)])


def roles(core, T, topo):
    me = T.rank_of(core)
    far = [s for s in range(N) if topo.chip(T.cores[s]) != topo.chip(core)]
    far.sort(key=lambda s: topo.die(T.cores[s]) != topo.die(core))
    return far + [s for s in range(N) if s != me and s not in far]


def rank_program(g, core, T, topo):
    me = T.rank_of(core)
    if me is None:
        return
    Q = {"V": g.vector, "S": g.scalar, "P": g.tensor, "G": g, "Y": g.sync}
    count = {"V": 0, "S": 0, "P": 0, "G": 0}
    seen = {}

    def wait(q, *toks):
        for name, val in toks:
            if seen.get((q, name), 0) < val:
                seen[(q, name)] = val
                Q[q].wait_ge(T.sem[name], val)

    def tick(q, ins):
        count[q] += 1
        ins.then_inc(T.sem[q], 1)
        return (q, count[q])

    def now(q):
        return (q, count[q])

    v, sc, pe, sy = g.vector, g.scalar, g.tensor, g.sync
    D = roles(core, T, topo)
    DM = D + [me]
    cores = T.cores
    A = AluOpType
    steps = [s.split(":") for s in PLAN.split()]
    names = [t for q, t in steps]
    own = len([t for t in names if t[0] == "o"])
    merged, wpe = "zo" not in names, "cw0" in names

    sc.dma_start(T.pk[:, 0:16], T.pick[:]).then_inc(T.sem.lpk, 16)
    col = {}
    nj = 0
    for k in (1, 2):
        col[k] = 4 * D[k]
        if MODE[k] == "V":
            col[k] = 16 + 4 * nj
            nj += 1
            for s in range(4):
                sy.dma_start(T.pk[32 * s:32 * s + 32, col[k]:col[k] + 4], T.pick[s:128:4, 4 * D[k]:4 * D[k] + 4]
                             ).then_inc(T.sem.lpj, 16)
    PK, PJ, LW = ("lpk", 16), ("lpj", 64 * nj), ("lw", 16 if wpe else 64)
    NX = 16 + 4 * nj

    t_ones = tick("V", v.memset(T.ones[:], 1.0))
    for l in "a" if merged else "oa":
        t_zero = tick("V", v.memset(T[l + "u"][:], 0.0))
    wait("G", t_ones)
    t_id = tick("G", g.affine_select(T.ident[:], T.ones[:], [[-1, 128]], A.is_equal, 0.0, 0, 1))

    wait("V", PK, PJ)
    tick("V", v.tensor_scalar(T.xa[:, 0:NX], T.pk[:, 0:NX], 0x180, None, A.bitwise_and))
    tick("V", v.tensor_scalar(T.xb[:, 0:NX], T.pk[:, 0:NX], 3, None, A.bitwise_and))
    tick("V", v.tensor_scalar(T.xk[:, 0:NX], T.pk[:, 0:NX], 2, 0x19F, A.arith_shift_right, A.bitwise_and))
    wait("V", now("V"))
    tick("V", v.tensor_scalar(T.x1[:, 0:NX], T.xa[:, 0:NX], 4.0, None, A.mult))
    tick("V", v.tensor_scalar(T.x2[:, 0:NX], T.xb[:, 0:NX], 32.0, None, A.mult))
    wait("V", now("V"))
    tick("V", v.tensor_tensor(T.x3[:, 0:NX], T.x1[:, 0:NX], T.x2[:, 0:NX], A.add))
    wait("V", now("V"))
    t_fx = tick("V", v.tensor_tensor(T.fx[:, 0:NX], T.x3[:, 0:NX], T.xk[:, 0:NX], A.add))

    eng = [topo.engines(core, cores[s]) for s in D]
    far = len(eng[0])
    picks = [eng[0][:far // 2], eng[1][far // 2:], [e for e in eng[2] if e not in eng[0]]]
    lanes = [eng[0], eng[1], picks[2]]

    def mask(es):
        return sum(1 << e for e in es)

    def transfer(k, src, dst):
        rid, pid, _ = topo.addr(cores[D[k]])
        return RemoteDMATransfer(dst_ids=[DstId(rid=rid, pnc=pid)], dma_engine_mask=mask(picks[k]),
                                 remote_sem=T.sem["list%d" % k], src=src, dst=dst)
    wait("G", PK)
    g.remote_dma_fused([transfer(0, T.pk[:, 4 * D[0]:4 * D[0] + 4], T.ld[:])], local_sem=T.sem.sent)
    wait("G", t_fx)
    g.remote_dma_fused([transfer(k, T.fx[:, col[k]:col[k] + 4], T.la[:, 4 * k - 4:4 * k]) for k in (1, 2)],
                       local_sem=T.sem.sent)
    LIST = [("list%d" % k, len(picks[k])) for k in range(3)]

    def gather(k, idx, t):
        g.indirect_dma_start(T["xg%d" % k][:, XC * t:XC * t + XC], None, T.x[:],
                             IndirectOffsetOnAxis(ap=idx, axis=0), bounds_check=R - 1).then_inc(T.sem["ig%d%d" % (k, t)], 16)

    def copy(q, out, in_):
        if q == "V":
            return tick("V", v.tensor_copy(out, in_))
        return tick("S", sc.activation(out, in_, COPY))

    def take(q, out, win, off):
        if q == "V":
            return tick("V", v.tensor_copy(out, win.indirect(off)))
        return tick("S", sc.activation(out, win.indirect(off), COPY))

    ob, o0 = ("a", 8) if merged else ("o", 0)
    ox = 8 * (o0 + 16) if wpe else 8 * (o0 + 4 * me)
    tok = {}
    ysum = [0]
    sent = [sum(len(e) for e in picks)]
    WSH = ("wsh", 64)
    turn = {"pX": 0, "pW": 0, "pY": 0}
    held, place = {}, {}
    calls = {k: 2 + len([t for t in names if t[:2] == "r" + k]) for k in "012"}
    gone = {k: 0 for k in "012"}

    def done(prefix, last=""):
        return [tok[t] for t in names if t.startswith(prefix) and t.endswith(last)]

    def gathered(k, t, b):
        return tok.get("g%sa%d" % (k, b)) or tok["g%s%d%d" % (k, t & 2, b)]

    def bank(ps, reader):
        b = turn[ps] % (T[ps].shape[1] // 512)
        turn[ps] += 1
        if (ps, b) in held:
            wait("P", tok[held[(ps, b)]])
        held[(ps, b)] = reader
        place[reader] = 512 * b
        return 512 * b

    def send(k, name, a, b):
        rid, pid, _ = topo.addr(cores[D[int(k)]])
        out, in_ = T["r" + name + k][:, a:b], T["x" + name + k][:, a:b]
        if name == "q":
            out, in_ = out.bitcast(dt.uint8), in_.bitcast(dt.uint8)
        g.remote_dma(out, in_, T.sem["arr" + k], T.sem.sent, pid, rid, mask(lanes[int(k)]))
        sent[0] += len(lanes[int(k)])

    def run(q, task):
        kind, k = task[0], task[1]
        i = int(task[-1]) if len(task) > 2 else 0
        if task[:2] == "lx":
            Q[q].dma_start(T.nat[:, 4 * i:4 * i + 4], T.x[512 * i:512 * i + 512, :]).then_inc(T.sem[task], 16)
        elif task[:2] == "tx":
            c, e = CHUNKS[task[2]]
            wait("V", *[("lx%d" % z, 16) for z in range(c, e)])
            for s in range(4):
                tok[task] = tick("V", v.transpose(T.stg[:, s, i, 128 * c:128 * e], T.nat[:, 4 * c:4 * e, i, :, s]))
        elif task[:2] == "ax":
            wait(q, *done("tx", task[2]))
            for a in range(4):
                Q[q].dma_start(T["xw%d" % i][:, 512 * a:512 * a + 512], T.stg[32 * a:32 * a + 32, :, i, :]
                               ).then_inc(T.sem["xsh%d" % i], 16)
        elif task == "lw" and wpe:
            Q[q].dma_start(T.wn[:], T.w[:]).then_inc(T.sem.lw, 16)
        elif task == "lw":
            for c in range(4):
                Q[q].dma_start(T.wn[:, 4 * c:4 * c + 4], T.w[512 * c:512 * c + 512, :]).then_inc(T.sem.lw, 16)
        elif task[:2] == "cw":
            wait(q, LW)
            tok[task] = copy(q, T.wf[:, 512 * i:512 * i + 512], T.wn[:, 4 * i:4 * i + 4])
        elif task[:2] == "tw" and wpe:
            wait("P", t_id, tok["cw%d" % i])
            b = bank("pW", "fw%d" % i)
            for t in range(4):
                o = 512 * i + 128 * t
                tok[task] = tick("P", pe.transpose(T.pW[:, b + 128 * t:b + 128 * t + 128], T.wf[:, o:o + 128], T.ident[:]))
        elif task[:2] == "fw":
            wait(q, tok["tw%d" % i])
            tok[task] = copy(q, T.ww[:, 512 * i:512 * i + 512], T.pW[:, place[task]:place[task] + 512])
        elif task == "pw":
            wait("V", t_fx)
            tick("V", v.tensor_scalar(T.xa[:, 0:16], T.pk[:, 0:16], 15, None, A.bitwise_and))
            tick("V", v.tensor_scalar(T.xk[:, 0:16], T.pk[:, 0:16], 4, None, A.arith_shift_right))
            wait("V", now("V"))
            tick("V", v.tensor_scalar(T.x1[:, 0:16], T.xa[:, 0:16], 128.0, None, A.mult))
            wait("V", now("V"))
            tok[task] = tick("V", v.tensor_tensor(T.fw[:], T.x1[:, 0:16], T.xk[:, 0:16], A.add))
        elif task == "tw":
            wait("V", LW)
            for b in range(4):
                tok[task] = tick("V", v.transpose(T.wst[:, b, :], T.wn[:, :, :, b]))
        elif task == "aw":
            wait(q, tok["tw"])
            for a in range(4):
                Q[q].dma_start(T.ww[:, 512 * a:512 * a + 512], T.wst[32 * a:32 * a + 32]).then_inc(T.sem.wsh, 16)
        elif kind == "u":
            wait(q, t_zero, *(LIST[1:3] if k == "a" else [tok["pw"] if wpe else t_fx]))
            for m in range(4):
                if k == "a":
                    t = copy(q, T.au[:, m, 0:8], T.la[:])
                else:
                    t = copy(q, T[ob + "u"][:, m, o0:o0 + 16], T.fw[:] if wpe else T.fx[:, 0:16])
                    if wpe and own < 4:
                        t = copy(q, T[ob + "u"][:, m, o0 + 16:o0 + 20], T.fx[:, 4 * me:4 * me + 4])
            if k == "o" and merged:
                tok["uo"] = tok["vo"] = t
            else:
                wait("P", t_id, t, *[tok["v" + u[1]] for u in tok if u[0] == "u"])
                tok[task] = tick("P", pe.transpose(T.pL[:, 0:128], T[k + "u"][:], T.ident[:]))
        elif kind == "v":
            wait(q, tok["u" + k])
            for d in range(2):
                tok[task] = copy(q, T[k + "v"][:, :, d, :], T.pL[:, 0:128])
        elif kind == "z":
            wait("V", tok["v" + k])
            for u in range(8):
                tick("V", v.transpose(T[k + "z"][:, :, u], T[k + "v"][:, u, :, :]))
            wait("V", now("V"))
            n = 8 if k == "a" and not merged else o0 + 16 + 4 * wpe
            tok[task] = tick("V", v.tensor_copy(T[k + "off"][:, 0:8 * n], T[k + "z"][:, 0:n, :]))
            if merged:
                tok["zo"] = tok[task]
        elif kind == "g" and k == "w":
            o = 8 * o0 + 32 * DM[i]
            wait(q, tok["zo"], *(done("fw") if wpe else [WSH]))
            tok[task] = take(q, T["gw%d" % i][:], T.ww[:], T[ob + "off"][:, o:o + 32])
        elif kind == "g":
            t, e = (0, 4) if task[2] == "a" else (int(task[2]), int(task[2]) + 2)
            o = 32 * int(k) - 32
            wait(q, tok["za"], ("xsh%d" % i, 64))
            out = T[("gb" if MODE[int(k)] == "V" else "gx") + k][:, i, 128 * t:128 * e]
            tok[task] = take(q, out, T["xw%d" % i][:], T.aoff[:, o + 8 * t:o + 8 * e])
        elif kind == "h":
            wait(q, tok["zo"], ("xsh" + k, 64))
            tok[task] = take(q, T.gx3[:, int(k), 128 * own:512], T["xw" + k][:], T[ob + "off"][:, ox + 8 * own:ox + 32])
        elif kind == "m":
            for t in range(4):
                wait("V", gathered(k, t, i))
                tok[task] = tick("V", v.transpose(T["mv" + k][:, :, i, :, t], T["gb" + k][:, i, 128 * t:128 * t + 128]))
        elif kind == "d":
            wait(q, *done("m" + k))
            for a in range(4):
                Q[q].dma_start(T["xt" + k][:, XC * a:XC * a + XC], T["mv" + k][32 * a:32 * a + 32]
                               ).then_inc(T.sem["xm" + k], 16)
        elif kind == "p" and k == "w":
            wait("P", t_id, tok["gw%d" % i])
            b = bank("pW", "ew%d" % i)
            for t in range(4):
                tok[task] = tick("P", pe.transpose(T.pW[:, b + t:b + 512:4], T["gw%d" % i][:, 128 * t:128 * t + 128], T.ident[:]))
        elif kind == "p" and k == "3":
            wait("P", t_id, *done("h"))
            o = bank("pX", "e3%d" % i)
            for b in range(3):
                tok[task] = tick("P", pe.transpose(T.pX[:, o + 128 * b:o + 128 * b + 128],
                                                   T.gx3[:, b, 128 * i:128 * i + 128], T.ident[:]))
        elif kind == "p":
            wait("P", t_id, gathered(k, 0, i))
            b = bank("pX", "e%s%d" % (k, i))
            for t in range(4):
                wait("P", gathered(k, t, i))
                tok[task] = tick("P", pe.transpose(T.pX[:, b + t:b + 512:4], T["gx" + k][:, i, 128 * t:128 * t + 128], T.ident[:]))
        elif kind == "e" and k == "w":
            wait(q, tok["pw%d" % i])
            tok[task] = copy(q, T.wt[:, 512 * i:512 * i + 512], T.pW[:, place[task]:place[task] + 512])
        elif kind == "e" and k == "3":
            wait(q, tok["p3%d" % i])
            tok[task] = copy(q, T.xt3[:, i:4 * XC:4], T.pX[:, place[task]:place[task] + XC])
        elif kind == "e":
            wait(q, tok["p%s%d" % (k, i)])
            tok[task] = copy(q, T["xt" + k][:, 512 * i:512 * i + 512], T.pX[:, place[task]:place[task] + 512])
        elif kind == "l":
            buf = "01"[k == "3"]
            wait(q, ("ig%s%d" % (buf, i), 16))
            tok[task] = copy(q, T["xt" + k][:, i:4 * XC:4], T["xg" + buf][:, XC * i:XC * i + XC])
        elif task == "qw":
            wait("V", *done("ew"))
            tok[task] = tick("V", v.quantize_mx(T.wq[:], T.ws[:], T.wt[:]))
        elif kind == "q" and len(task) == 3:
            n = {"w": "w%s", "1": "x%s1", "2": "x%s2"}[k]
            wait("V", tok["e" + task[1:]])
            tok[task] = tick("V", v.quantize_mx(T[n % "q"][:, 128 * i:128 * i + 128], T[n % "s"][:, 128 * i:128 * i + 128],
                                                T[n % "t"][:, 512 * i:512 * i + 512]))
        elif kind == "q":
            wait("V", *([("xm" + k, 64)] if MODE.get(int(k)) == "V" else done("l" + k) + done("e" + k)))
            tok[task] = tick("V", v.quantize_mx(T["xq" + k][:], T["xs" + k][:], T["xt" + k][:]))
        elif kind == "o":
            t = int(k)
            gather(1, T.pk[:, 4 * me + t:4 * me + t + 1], t)
        elif kind == "i":
            wait("G", LIST[0])
            gather(0, T.ld[:, int(k):int(k) + 1], int(k))
        elif kind == "r":
            wait("G", *[tok["q%s%d" % (k, b)] for b in range(i + 1)])
            send(k, "q", gone[k], 128 * i + 128)
            gone[k] = 128 * i + 128
        elif kind == "s":
            wait("G", *done("q" + k))
            send(k, "q", gone[k], XC)
            send(k, "s", 0, XC)
        elif kind == "y":
            j = int(k)
            s = DM[j]
            if k == "3":
                xq, xs, arrived = T.xq3, T.xs3, tok["q3"]
            else:
                xq, xs, arrived = T["rq" + k], T["rs" + k], ("arr" + k, calls[k] * len(lanes[j]))
            wait("P", tok["qw"] if "qw" in tok else tok["qw" + k], arrived)
            b = bank("pY", task)
            m = tick("P", pe.matmul_mx(T.pY[:, b:b + XC], T.wq[:, 128 * j:128 * j + 128],
                                       T.ws[:, 128 * j:128 * j + 128], xq[:], xs[:], True, True))
            wait(q, m)
            if MODE.get(j) != "V":
                tok[task] = copy(q, T.ysb[:, s], T.pY[:, b:b + XC])
            else:
                for a in range(4):
                    tok[task] = copy(q, T.ysb[:, s, :, a, :], T.pY[:, b + 96 * a:b + 96 * a + 96])
            wait("Y", tok[task])
            sy.dma_start(T.y[:, XC * s:XC * s + XC], T.ysb[:, s]).then_inc(T.sem["ys%d" % ysum[0]], 16)
            ysum[0] += 1

    for q, task in steps:
        run(q, task)
    for i in range(4):
        wait("Y", ("ys%d" % i, 16))
    wait("Y", now("V"), now("S"), now("P"), now("G"))
    wait("G", ("sent", sent[0]))
